import numpy as np, ml_dtypes
CORES = [51,54,179,182]
N = 4
import mx_ref
NC, KT, G, WT = 256, 1, 4, 1
C = np.float32(0.043)
BF = ml_dtypes.bfloat16
def cut(t, i, w=512):
    return t[:, w * i:w * i + w]
def tile(rs):
    return np.stack(rs, axis=2).reshape(128, -1).astype(BF)
def layer(w, X):
    out = []
    for i in range(G):
        for t in range(len(X)):
            p = mx_ref.matmul(mx_ref.quantize(cut(w, len(X) * i + t)), X[t])
            z = p if t == 0 else z + p
        out.append(z)
    return out
def act(Z):
    return [np.maximum(z, 0) * C for z in Z]
def setup_inputs(rng):
    def f(*shape):
        return mx_ref.flush((rng.standard_normal(shape, dtype=np.float32) * np.exp2(rng.integers(-2, 3, shape[:-1] + (1,)))).astype(BF))
    return {"x": f(N, 128, KT * 4 * NC), "w1": f(N, 128, G * KT * 512), "w2": f(N, 128, WT * 512)}
def setup_inputs_blocks(rng):
    d = setup_inputs(rng)
    for k in ("x", "w1", "w2"): d[k] = mx_ref.spread(d[k], rng, 4)
    return d
def setup_inputs_wide(rng):
    d = setup_inputs(rng)
    for k in ("x", "w1", "w2"): d[k] = mx_ref.flush((d[k].astype(np.float32) * np.exp2(rng.integers(-8, 9, (N, 1, 1))).astype(np.float32)).astype(BF))
    return d
def setup_inputs_zeros(rng):
    d = setup_inputs(rng); v = d["x"].reshape(N, 128, -1, 4).copy()
    v[np.broadcast_to((rng.random((N, 1, v.shape[2], 1)) < 0.33), v.shape)] = 0
    d["x"] = v.reshape(d["x"].shape)
    return d
def reference(x, w1, w2):
    H = [mx_ref.quantize(tile(act(layer(w1[j], [mx_ref.quantize(cut(x[j], t, 4 * NC)) for t in range(KT)])))) for j in range(N)]
    y = np.zeros((N, 128, N * WT * NC), np.float32)
    for r in range(N):
        for i in range(WT):
            qw = mx_ref.quantize(cut(w2[r], i))
            for j in range(N):
                y[r][:, NC * (WT * j + i):NC * (WT * j + i) + NC] = mx_ref.matmul(qw, H[j])
    return {"y": y}

@@ -1,0 +1,139 @@
+import numpy as np
+from concourse.mybir import dt, AluOpType, ActivationFunctionType
+
+COLS = 256
+HALF = 128
+ST = 128
+C = float(np.float32(0.043))
+BANK = 512
+
+CODE, BYTE = "float8_e4m3fn_x4", "uint8"
+SCRATCH = {
+    "xb": ("sbuf", [128, 1024], "bfloat16"),
+    "w1b": ("sbuf", [128, 2048], "bfloat16"),
+    "w2b": ("sbuf", [128, 512], "bfloat16"),
+    "hb": ("sbuf", [128, 1024], "bfloat16"),
+    "yb": ("sbuf", [128, 1024], "float32"),
+    "xc": ("sbuf", [128, COLS], CODE), "xs": ("sbuf", [128, COLS], BYTE),
+    "w1c": ("sbuf", [128, 4 * ST], CODE), "w1s": ("sbuf", [128, 4 * ST], BYTE),
+    "w2c": ("sbuf", [128, ST], CODE), "w2s": ("sbuf", [128, ST], BYTE),
+    "hc": ("sbuf", [128, COLS], CODE), "hs": ("sbuf", [128, COLS], BYTE),
+    "pc": ("sbuf", [128, COLS], CODE), "ps": ("sbuf", [128, COLS], BYTE),
+    "ac": ("sbuf", [128, COLS], CODE), "asc": ("sbuf", [128, COLS], BYTE),
+    "oc": ("sbuf", [128, COLS], CODE), "osc": ("sbuf", [128, COLS], BYTE),
+    "acc": ("psum", [128, 8 * BANK], "float32"),
+}
+SEMAPHORES = ["ldx", "ldw", "ldw3", "ldw2", "qx", "q0", "q1", "q2", "q3", "qv",
+              "m0", "m1", "m2", "m3a", "m3b", "acta", "actb", "hq",
+              "sent", "arrc", "arrs", "arrp", "arro",
+              "mo", "mp", "ma", "mfa", "mfb", "co", "cp", "ca", "cf", "st"]
+
+
+def rank_program(g, core, T, topo):
+    if T.rank_of(core) is None:
+        return
+    s = T.sem
+    relu, copy = ActivationFunctionType.Relu, ActivationFunctionType.Copy
+    others = [c for c in T.cores if c != core]
+    partner = [c for c in others if topo.host(c) == topo.host(core) and topo.chip(c) == topo.chip(core)][0]
+    across = [c for c in others if topo.host(c) != topo.host(core) and topo.die(c) == topo.die(core)][0]
+    far = [c for c in others if c not in (partner, across)][0]
+
+    def bank(b, n=COLS):
+        return T.acc[:, b * BANK:b * BANK + n]
+
+    def yblock(c, a=0, b=COLS):
+        k = COLS * T.rank_of(c)
+        return slice(k + a, k + b)
+
+    g.sync.dma_start(T.xb[:], T.x[:]).then_inc(s.ldx, 16)
+    g.scalar.dma_start(T.w1b[:, 0:1536], T.w1[:, 0:1536]).then_inc(s.ldw, 16)
+    g.sync.dma_start(T.w1b[:, 1536:2048], T.w1[:, 1536:2048]).then_inc(s.ldw3, 16)
+    g.scalar.wait_ge(s.ldx, 16)
+    g.scalar.dma_start(T.w2b[:], T.w2[:]).then_inc(s.ldw2, 16)
+
+    v = g.vector
+    v.wait_ge(s.ldx, 16)
+    v.quantize_mx(T.xc[:], T.xs[:], T.xb[:]).then_inc(s.qx, 1)
+    v.wait_ge(s.ldw, 16)
+    for i in range(4):
+        if i == 3:
+            v.wait_ge(s.ldw3, 16)
+        v.quantize_mx(T.w1c[:, ST * i:ST * i + ST], T.w1s[:, ST * i:ST * i + ST],
+                      T.w1b[:, 512 * i:512 * i + 512]).then_inc(s["q%d" % i], 1)
+
+    t = g.tensor
+    t.wait_ge(s.qx, 1)
+    for i in range(3):
+        t.wait_ge(s["q%d" % i], 1)
+        t.matmul_mx(bank(i), T.w1c[:, ST * i:ST * i + ST], T.w1s[:, ST * i:ST * i + ST],
+                    T.xc[:], T.xs[:], True, True).then_inc(s["m%d" % i], 1)
+    t.wait_ge(s.q3, 1)
+    for b, a, sem in ((3, 0, s.m3a), (4, HALF, s.m3b)):
+        t.matmul_mx(bank(b, HALF), T.w1c[:, 3 * ST:4 * ST], T.w1s[:, 3 * ST:4 * ST],
+                    T.xc[:, a:a + HALF], T.xs[:, a:a + HALF], True, True).then_inc(sem, 1)
+
+    for i in range(3):
+        g.scalar.wait_ge(s["m%d" % i], 1)
+        g.scalar.activation(T.hb[:, i:4 * COLS:4], bank(i), relu, scale=C).then_inc(s.acta, 1)
+    g.scalar.wait_ge(s.m3b, 1)
+    g.scalar.activation(T.hb[:, 4 * HALF + 3:4 * COLS:4], bank(4, HALF), relu, scale=C).then_inc(s.actb, 1)
+    v.wait_ge(s.m3a, 1)
+    v.tensor_scalar(T.hb[:, 3:4 * HALF:4], bank(3, HALF), 0.0, C, AluOpType.max, AluOpType.mult).then_inc(s.acta, 1)
+    v.wait_ge(s.acta, 4)
+    v.quantize_mx(T.hc[:, 0:HALF], T.hs[:, 0:HALF], T.hb[:, 0:4 * HALF]).then_inc(s.hq, 1)
+    v.wait_ge(s.actb, 1)
+    v.quantize_mx(T.hc[:, HALF:COLS], T.hs[:, HALF:COLS], T.hb[:, 4 * HALF:4 * COLS]).then_inc(s.hq, 1)
+    v.wait_ge(s.ldw2, 16)
+    v.quantize_mx(T.w2c[:], T.w2s[:], T.w2b[:]).then_inc(s.qv, 1)
+
+    out_mask = topo.mask(core, across)
+    chip_mask = topo.mask(core, partner)
+    rest_mask = chip_mask & ~out_mask
+    n_out, n_chip, n_rest = [bin(m).count("1") for m in (out_mask, chip_mask, rest_mask)]
+
+    def send(dst, out, src, sem, mask):
+        rid, pid = topo.addr(dst, core)
+        g.remote_dma(out_ap=out, in_ap=src, remote_sem=sem, local_sem=s.sent, pid=pid, routing_id=rid,
+                     dma_engine_mask=mask)
+
+    u8 = dt.uint8
+    g.wait_ge(s.hq, 2)
+    send(across, T.ac[:].bitcast(u8), T.hc[:].bitcast(u8), s.arrc, out_mask)
+    send(across, T.asc[:], T.hs[:], s.arrs, out_mask)
+    send(partner, T.pc[:].bitcast(u8), T.hc[:].bitcast(u8), s.arrp, rest_mask)
+    send(partner, T.ps[:], T.hs[:], s.arrp, rest_mask)
+    g.wait_ge(s.arrc, n_out)
+    send(partner, T.oc[:].bitcast(u8), T.ac[:].bitcast(u8), s.arro, chip_mask)
+    g.wait_ge(s.arrs, n_out)
+    send(partner, T.osc[:], T.asc[:], s.arro, chip_mask)
+    g.wait_ge(s.sent, 2 * (n_out + n_rest + n_chip))
+
+    t.wait_ge(s.hq, 2)
+    t.wait_ge(s.qv, 1)
+    t.matmul_mx(bank(5), T.w2c[:], T.w2s[:], T.hc[:], T.hs[:], True, True).then_inc(s.mo, 1)
+    t.wait_ge(s.arrp, 2 * n_rest)
+    t.matmul_mx(bank(6), T.w2c[:], T.w2s[:], T.pc[:], T.ps[:], True, True).then_inc(s.mp, 1)
+    t.wait_ge(s.arrc, n_out)
+    t.wait_ge(s.arrs, n_out)
+    t.matmul_mx(bank(7), T.w2c[:], T.w2s[:], T.ac[:], T.asc[:], True, True).then_inc(s.ma, 1)
+    t.wait_ge(s.arro, 2 * n_chip)
+    for b, a, sem in ((0, 0, s.mfa), (1, HALF, s.mfb)):
+        t.matmul_mx(bank(b, HALF), T.w2c[:], T.w2s[:], T.oc[:, a:a + HALF], T.osc[:, a:a + HALF],
+                    True, True).then_inc(sem, 1)
+
+    v.wait_ge(s.mo, 1)
+    v.tensor_copy(T.yb[:, yblock(core)], bank(5)).then_inc(s.co, 1)
+    g.scalar.wait_ge(s.mp, 1)
+    g.scalar.activation(T.yb[:, yblock(partner)], bank(6), copy).then_inc(s.cp, 1)
+    v.wait_ge(s.ma, 1)
+    v.tensor_copy(T.yb[:, yblock(across)], bank(7)).then_inc(s.ca, 1)
+    g.scalar.wait_ge(s.mfa, 1)
+    g.scalar.activation(T.yb[:, yblock(far, 0, HALF)], bank(0, HALF), copy).then_inc(s.cf, 1)
+    v.wait_ge(s.mfb, 1)
+    v.tensor_copy(T.yb[:, yblock(far, HALF, COLS)], bank(1, HALF)).then_inc(s.cf, 1)
+
+    for c, sem, n in ((core, s.co, 1), (partner, s.cp, 1), (across, s.ca, 1), (far, s.cf, 2)):
+        g.sync.wait_ge(sem, n)
+        g.sync.dma_start(T.y[:, yblock(c)], T.yb[:, yblock(c)]).then_inc(s.st, 16)
+    g.sync.wait_ge(s.st, 64)

@@ -1,4 +1,5 @@
 import numpy as np
+from concourse.bass import DstId, RemoteDMATransfer
 from concourse.mybir import dt, AluOpType, ActivationFunctionType
 
 COLS = 256
@@ -23,10 +24,8 @@ SCRATCH = {
     "oc": ("sbuf", [128, COLS], CODE), "osc": ("sbuf", [128, COLS], BYTE),
     "acc": ("psum", [128, 8 * BANK], "float32"),
 }
-SEMAPHORES = ["ldx", "ldw", "ldw3", "ldw2", "qx", "q0", "q1", "q2", "q3", "qv",
-              "m0", "m1", "m2", "m3a", "m3b", "acta", "actb", "hq",
-              "sent", "arrc", "arrs", "arrp", "arro",
-              "mo", "mp", "ma", "mfa", "mfb", "co", "cp", "ca", "cf", "st"]
+SEMAPHORES = (["ldw", "ldw3", "ldw2", "q0", "q1", "q2", "q3", "qv", "sent", "arrs", "arrp", "mo", "mp", "mc", "co", "cp", "cc", "st"]
+              + [n + k for k in "ab" for n in ("ldx", "qx", "m0", "m1", "m2", "m3", "act", "hq", "arr", "onw", "mf", "cf")])
 
 
 def rank_program(g, core, T, topo):
@@ -38,6 +37,8 @@ def rank_program(g, core, T, topo):
     partner = [c for c in others if topo.host(c) == topo.host(core) and topo.chip(c) == topo.chip(core)][0]
     across = [c for c in others if topo.host(c) != topo.host(core) and topo.die(c) == topo.die(core)][0]
     far = [c for c in others if c not in (partner, across)][0]
+    halves = (("a", 0, HALF, 0), ("b", HALF, COLS, 4))
+    v, t = g.vector, g.tensor
 
     def bank(b, n=COLS):
         return T.acc[:, b * BANK:b * BANK + n]
@@ -46,48 +47,53 @@ def rank_program(g, core, T, topo):
         k = COLS * T.rank_of(c)
         return slice(k + a, k + b)
 
-    g.sync.dma_start(T.xb[:], T.x[:]).then_inc(s.ldx, 16)
+    g.sync.dma_start(T.xb[:, 0:512], T.x[:, 0:512]).then_inc(s.ldxa, 16)
     g.scalar.dma_start(T.w1b[:, 0:1536], T.w1[:, 0:1536]).then_inc(s.ldw, 16)
     g.sync.dma_start(T.w1b[:, 1536:2048], T.w1[:, 1536:2048]).then_inc(s.ldw3, 16)
-    g.scalar.wait_ge(s.ldx, 16)
+    g.sync.dma_start(T.xb[:, 512:1024], T.x[:, 512:1024]).then_inc(s.ldxb, 16)
+    g.scalar.wait_ge(s.ldxa, 16)
     g.scalar.dma_start(T.w2b[:], T.w2[:]).then_inc(s.ldw2, 16)
 
-    v = g.vector
-    v.wait_ge(s.ldx, 16)
-    v.quantize_mx(T.xc[:], T.xs[:], T.xb[:]).then_inc(s.qx, 1)
-    v.wait_ge(s.ldw, 16)
-    for i in range(4):
-        if i == 3:
-            v.wait_ge(s.ldw3, 16)
+    def quant_x(k, a, b):
+        v.wait_ge(s["ldx" + k], 16)
+        v.quantize_mx(T.xc[:, a:b], T.xs[:, a:b], T.xb[:, 4 * a:4 * b]).then_inc(s["qx" + k], 1)
+
+    def quant_w1(i):
         v.quantize_mx(T.w1c[:, ST * i:ST * i + ST], T.w1s[:, ST * i:ST * i + ST],
                       T.w1b[:, 512 * i:512 * i + 512]).then_inc(s["q%d" % i], 1)
 
-    t = g.tensor
-    t.wait_ge(s.qx, 1)
-    for i in range(3):
-        t.wait_ge(s["q%d" % i], 1)
-        t.matmul_mx(bank(i), T.w1c[:, ST * i:ST * i + ST], T.w1s[:, ST * i:ST * i + ST],
-                    T.xc[:], T.xs[:], True, True).then_inc(s["m%d" % i], 1)
-    t.wait_ge(s.q3, 1)
-    for b, a, sem in ((3, 0, s.m3a), (4, HALF, s.m3b)):
-        t.matmul_mx(bank(b, HALF), T.w1c[:, 3 * ST:4 * ST], T.w1s[:, 3 * ST:4 * ST],
-                    T.xc[:, a:a + HALF], T.xs[:, a:a + HALF], True, True).then_inc(sem, 1)
+    def finish_h(k, a, b, bk):
+        v.wait_ge(s["m3" + k], 1)
+        v.tensor_scalar(T.hb[:, 4 * a + 3:4 * b:4], bank(bk + 3, HALF), 0.0, C,
+                        AluOpType.max, AluOpType.mult).then_inc(s["act" + k], 1)
+        v.wait_ge(s["act" + k], 4)
+        v.quantize_mx(T.hc[:, a:b], T.hs[:, a:b], T.hb[:, 4 * a:4 * b]).then_inc(s["hq" + k], 1)
 
+    quant_x("a", 0, HALF)
+    v.wait_ge(s.ldw, 16)
     for i in range(3):
-        g.scalar.wait_ge(s["m%d" % i], 1)
-        g.scalar.activation(T.hb[:, i:4 * COLS:4], bank(i), relu, scale=C).then_inc(s.acta, 1)
-    g.scalar.wait_ge(s.m3b, 1)
-    g.scalar.activation(T.hb[:, 4 * HALF + 3:4 * COLS:4], bank(4, HALF), relu, scale=C).then_inc(s.actb, 1)
-    v.wait_ge(s.m3a, 1)
-    v.tensor_scalar(T.hb[:, 3:4 * HALF:4], bank(3, HALF), 0.0, C, AluOpType.max, AluOpType.mult).then_inc(s.acta, 1)
-    v.wait_ge(s.acta, 4)
-    v.quantize_mx(T.hc[:, 0:HALF], T.hs[:, 0:HALF], T.hb[:, 0:4 * HALF]).then_inc(s.hq, 1)
-    v.wait_ge(s.actb, 1)
-    v.quantize_mx(T.hc[:, HALF:COLS], T.hs[:, HALF:COLS], T.hb[:, 4 * HALF:4 * COLS]).then_inc(s.hq, 1)
+        quant_w1(i)
+    v.wait_ge(s.ldw3, 16)
+    quant_w1(3)
+    finish_h(*halves[0])
+    quant_x("b", HALF, COLS)
+    finish_h(*halves[1])
     v.wait_ge(s.ldw2, 16)
     v.quantize_mx(T.w2c[:], T.w2s[:], T.w2b[:]).then_inc(s.qv, 1)
 
-    out_mask = topo.mask(core, across)
+    for k, a, b, bk in halves:
+        t.wait_ge(s["qx" + k], 1)
+        for i in range(4):
+            if k == "a":
+                t.wait_ge(s["q%d" % i], 1)
+            t.matmul_mx(bank(bk + i, HALF), T.w1c[:, ST * i:ST * i + ST], T.w1s[:, ST * i:ST * i + ST],
+                        T.xc[:, a:b], T.xs[:, a:b], True, True).then_inc(s["m%d%s" % (i, k)], 1)
+        for i in range(3):
+            g.scalar.wait_ge(s["m%d%s" % (i, k)], 1)
+            g.scalar.activation(T.hb[:, 4 * a + i:4 * b:4], bank(bk + i, HALF), relu,
+                                scale=C).then_inc(s["act" + k], 1)
+
+    out_mask = topo.mask(core, across) & topo.mask(core, far)
     chip_mask = topo.mask(core, partner)
     rest_mask = chip_mask & ~out_mask
     n_out, n_chip, n_rest = [bin(m).count("1") for m in (out_mask, chip_mask, rest_mask)]
@@ -97,43 +103,52 @@ def rank_program(g, core, T, topo):
         g.remote_dma(out_ap=out, in_ap=src, remote_sem=sem, local_sem=s.sent, pid=pid, routing_id=rid,
                      dma_engine_mask=mask)
 
+    def dst_id(c):
+        rid, pid = topo.addr(c, core)
+        return DstId(rid=rid, pnc=pid)
+
     u8 = dt.uint8
-    g.wait_ge(s.hq, 2)
-    send(across, T.ac[:].bitcast(u8), T.hc[:].bitcast(u8), s.arrc, out_mask)
-    send(across, T.asc[:], T.hs[:], s.arrs, out_mask)
+    for k, a, b, bk in halves:
+        g.wait_ge(s["hq" + k], 1)
+        send(across, T.ac[:, a:b].bitcast(u8), T.hc[:, a:b].bitcast(u8), s["arr" + k], out_mask)
+    g.remote_dma_fused([RemoteDMATransfer(dst_ids=[dst_id(across), dst_id(far)], dma_engine_mask=out_mask,
+                                          remote_sem=s.arrs, srcs=[T.hs[:]], dsts=[T.asc[:], T.osc[:]])],
+                       local_sem=s.sent)
     send(partner, T.pc[:].bitcast(u8), T.hc[:].bitcast(u8), s.arrp, rest_mask)
     send(partner, T.ps[:], T.hs[:], s.arrp, rest_mask)
-    g.wait_ge(s.arrc, n_out)
-    send(partner, T.oc[:].bitcast(u8), T.ac[:].bitcast(u8), s.arro, chip_mask)
-    g.wait_ge(s.arrs, n_out)
-    send(partner, T.osc[:], T.asc[:], s.arro, chip_mask)
-    g.wait_ge(s.sent, 2 * (n_out + n_rest + n_chip))
+    for k, a, b, bk in halves:
+        g.wait_ge(s["arr" + k], n_out)
+        send(partner, T.oc[:, a:b].bitcast(u8), T.ac[:, a:b].bitcast(u8), s["onw" + k], chip_mask)
+    g.wait_ge(s.sent, 3 * n_out + 2 * n_rest + 2 * n_chip)
 
-    t.wait_ge(s.hq, 2)
+    t.wait_ge(s.hqa, 1)
+    t.wait_ge(s.hqb, 1)
     t.wait_ge(s.qv, 1)
-    t.matmul_mx(bank(5), T.w2c[:], T.w2s[:], T.hc[:], T.hs[:], True, True).then_inc(s.mo, 1)
+    t.matmul_mx(bank(0), T.w2c[:], T.w2s[:], T.hc[:], T.hs[:], True, True).then_inc(s.mo, 1)
     t.wait_ge(s.arrp, 2 * n_rest)
-    t.matmul_mx(bank(6), T.w2c[:], T.w2s[:], T.pc[:], T.ps[:], True, True).then_inc(s.mp, 1)
-    t.wait_ge(s.arrc, n_out)
-    t.wait_ge(s.arrs, n_out)
-    t.matmul_mx(bank(7), T.w2c[:], T.w2s[:], T.ac[:], T.asc[:], True, True).then_inc(s.ma, 1)
-    t.wait_ge(s.arro, 2 * n_chip)
-    for b, a, sem in ((0, 0, s.mfa), (1, HALF, s.mfb)):
-        t.matmul_mx(bank(b, HALF), T.w2c[:], T.w2s[:], T.oc[:, a:a + HALF], T.osc[:, a:a + HALF],
-                    True, True).then_inc(sem, 1)
+    t.matmul_mx(bank(1), T.w2c[:], T.w2s[:], T.pc[:], T.ps[:], True, True).then_inc(s.mp, 1)
+    t.wait_ge(s.arra, n_out)
+    t.wait_ge(s.arrb, n_out)
+    t.wait_ge(s.arrs, 2 * n_out)
+    t.matmul_mx(bank(2), T.w2c[:], T.w2s[:], T.ac[:], T.asc[:], True, True).then_inc(s.mc, 1)
+    for k, a, b, bk in halves:
+        t.wait_ge(s["onw" + k], n_chip)
+        t.matmul_mx(bank(3 + bk, HALF), T.w2c[:], T.w2s[:], T.oc[:, a:b], T.osc[:, a:b],
+                    True, True).then_inc(s["mf" + k], 1)
 
     v.wait_ge(s.mo, 1)
-    v.tensor_copy(T.yb[:, yblock(core)], bank(5)).then_inc(s.co, 1)
+    v.tensor_copy(T.yb[:, yblock(core)], bank(0)).then_inc(s.co, 1)
     g.scalar.wait_ge(s.mp, 1)
-    g.scalar.activation(T.yb[:, yblock(partner)], bank(6), copy).then_inc(s.cp, 1)
-    v.wait_ge(s.ma, 1)
-    v.tensor_copy(T.yb[:, yblock(across)], bank(7)).then_inc(s.ca, 1)
+    g.scalar.activation(T.yb[:, yblock(partner)], bank(1), copy).then_inc(s.cp, 1)
+    v.wait_ge(s.mc, 1)
+    v.tensor_copy(T.yb[:, yblock(across)], bank(2)).then_inc(s.cc, 1)
     g.scalar.wait_ge(s.mfa, 1)
-    g.scalar.activation(T.yb[:, yblock(far, 0, HALF)], bank(0, HALF), copy).then_inc(s.cf, 1)
+    g.scalar.activation(T.yb[:, yblock(far, 0, HALF)], bank(3, HALF), copy).then_inc(s.cfa, 1)
     v.wait_ge(s.mfb, 1)
-    v.tensor_copy(T.yb[:, yblock(far, HALF, COLS)], bank(1, HALF)).then_inc(s.cf, 1)
+    v.tensor_copy(T.yb[:, yblock(far, HALF, COLS)], bank(7, HALF)).then_inc(s.cfb, 1)
 
-    for c, sem, n in ((core, s.co, 1), (partner, s.cp, 1), (across, s.ca, 1), (far, s.cf, 2)):
-        g.sync.wait_ge(sem, n)
-        g.sync.dma_start(T.y[:, yblock(c)], T.yb[:, yblock(c)]).then_inc(s.st, 16)
-    g.sync.wait_ge(s.st, 64)
+    for sem, cols in ((s.co, yblock(core)), (s.cp, yblock(partner)), (s.cc, yblock(across)),
+                      (s.cfa, yblock(far, 0, HALF)), (s.cfb, yblock(far, HALF, COLS))):
+        g.sync.wait_ge(sem, 1)
+        g.sync.dma_start(T.y[:, cols], T.yb[:, cols]).then_inc(s.st, 16)
+    g.sync.wait_ge(s.st, 80)

import numpy as np
from concourse.bass import DstId, RemoteDMATransfer
from concourse.mybir import dt, AluOpType, ActivationFunctionType

COLS = 256
HALF = 128
ST = 128
C = float(np.float32(0.043))
BANK = 512

CODE, BYTE = "float8_e4m3fn_x4", "uint8"
SCRATCH = {
    "xb": ("sbuf", [128, 1024], "bfloat16"),
    "w1b": ("sbuf", [128, 2048], "bfloat16"),
    "w2b": ("sbuf", [128, 512], "bfloat16"),
    "hb": ("sbuf", [128, 1024], "bfloat16"),
    "yb": ("sbuf", [128, 1024], "float32"),
    "xc": ("sbuf", [128, COLS], CODE), "xs": ("sbuf", [128, COLS], BYTE),
    "w1c": ("sbuf", [128, 4 * ST], CODE), "w1s": ("sbuf", [128, 4 * ST], BYTE),
    "w2c": ("sbuf", [128, ST], CODE), "w2s": ("sbuf", [128, ST], BYTE),
    "hc": ("sbuf", [128, COLS], CODE), "hs": ("sbuf", [128, COLS], BYTE),
    "pc": ("sbuf", [128, COLS], CODE), "ps": ("sbuf", [128, COLS], BYTE),
    "ac": ("sbuf", [128, COLS], CODE), "asc": ("sbuf", [128, COLS], BYTE),
    "oc": ("sbuf", [128, COLS], CODE), "osc": ("sbuf", [128, COLS], BYTE),
    "acc": ("psum", [128, 8 * BANK], "float32"),
}
SEMAPHORES = (["ldw", "ldw3", "ldw2", "q0", "q1", "q2", "q3", "qv", "sent", "arrs", "arrp", "mo", "mp", "mc", "co", "cp", "cc", "st"]
              + [n + k for k in "ab" for n in ("ldx", "qx", "m0", "m1", "m2", "m3", "act", "hq", "arr", "onw", "mf", "cf")])


def rank_program(g, core, T, topo):
    if T.rank_of(core) is None:
        return
    s = T.sem
    relu, copy = ActivationFunctionType.Relu, ActivationFunctionType.Copy
    others = [c for c in T.cores if c != core]
    partner = [c for c in others if topo.host(c) == topo.host(core) and topo.chip(c) == topo.chip(core)][0]
    across = [c for c in others if topo.host(c) != topo.host(core) and topo.die(c) == topo.die(core)][0]
    far = [c for c in others if c not in (partner, across)][0]
    halves = (("a", 0, HALF, 0), ("b", HALF, COLS, 4))
    v, t = g.vector, g.tensor

    def bank(b, n=COLS):
        return T.acc[:, b * BANK:b * BANK + n]

    def yblock(c, a=0, b=COLS):
        k = COLS * T.rank_of(c)
        return slice(k + a, k + b)

    g.sync.dma_start(T.xb[:, 0:512], T.x[:, 0:512]).then_inc(s.ldxa, 16)
    g.scalar.dma_start(T.w1b[:, 0:1536], T.w1[:, 0:1536]).then_inc(s.ldw, 16)
    g.sync.dma_start(T.w1b[:, 1536:2048], T.w1[:, 1536:2048]).then_inc(s.ldw3, 16)
    g.sync.dma_start(T.xb[:, 512:1024], T.x[:, 512:1024]).then_inc(s.ldxb, 16)
    g.scalar.wait_ge(s.ldxa, 16)
    g.scalar.dma_start(T.w2b[:], T.w2[:]).then_inc(s.ldw2, 16)

    def quant_x(k, a, b):
        v.wait_ge(s["ldx" + k], 16)
        v.quantize_mx(T.xc[:, a:b], T.xs[:, a:b], T.xb[:, 4 * a:4 * b]).then_inc(s["qx" + k], 1)

    def quant_w1(i):
        v.quantize_mx(T.w1c[:, ST * i:ST * i + ST], T.w1s[:, ST * i:ST * i + ST],
                      T.w1b[:, 512 * i:512 * i + 512]).then_inc(s["q%d" % i], 1)

    def finish_h(k, a, b, bk):
        v.wait_ge(s["m3" + k], 1)
        v.tensor_scalar(T.hb[:, 4 * a + 3:4 * b:4], bank(bk + 3, HALF), 0.0, C,
                        AluOpType.max, AluOpType.mult).then_inc(s["act" + k], 1)
        v.wait_ge(s["act" + k], 4)
        v.quantize_mx(T.hc[:, a:b], T.hs[:, a:b], T.hb[:, 4 * a:4 * b]).then_inc(s["hq" + k], 1)

    quant_x("a", 0, HALF)
    v.wait_ge(s.ldw, 16)
    for i in range(3):
        quant_w1(i)
    v.wait_ge(s.ldw3, 16)
    quant_w1(3)
    finish_h(*halves[0])
    quant_x("b", HALF, COLS)
    finish_h(*halves[1])
    v.wait_ge(s.ldw2, 16)
    v.quantize_mx(T.w2c[:], T.w2s[:], T.w2b[:]).then_inc(s.qv, 1)

    for k, a, b, bk in halves:
        t.wait_ge(s["qx" + k], 1)
        for i in range(4):
            if k == "a":
                t.wait_ge(s["q%d" % i], 1)
            t.matmul_mx(bank(bk + i, HALF), T.w1c[:, ST * i:ST * i + ST], T.w1s[:, ST * i:ST * i + ST],
                        T.xc[:, a:b], T.xs[:, a:b], True, True).then_inc(s["m%d%s" % (i, k)], 1)
        for i in range(3):
            g.scalar.wait_ge(s["m%d%s" % (i, k)], 1)
            g.scalar.activation(T.hb[:, 4 * a + i:4 * b:4], bank(bk + i, HALF), relu,
                                scale=C).then_inc(s["act" + k], 1)

    out_mask = topo.mask(core, across) & topo.mask(core, far)
    chip_mask = topo.mask(core, partner)
    rest_mask = chip_mask & ~out_mask
    n_out, n_chip, n_rest = [bin(m).count("1") for m in (out_mask, chip_mask, rest_mask)]

    def send(dst, out, src, sem, mask):
        rid, pid = topo.addr(dst, core)
        g.remote_dma(out_ap=out, in_ap=src, remote_sem=sem, local_sem=s.sent, pid=pid, routing_id=rid,
                     dma_engine_mask=mask)

    def dst_id(c):
        rid, pid = topo.addr(c, core)
        return DstId(rid=rid, pnc=pid)

    u8 = dt.uint8
    for k, a, b, bk in halves:
        g.wait_ge(s["hq" + k], 1)
        send(across, T.ac[:, a:b].bitcast(u8), T.hc[:, a:b].bitcast(u8), s["arr" + k], out_mask)
    g.remote_dma_fused([RemoteDMATransfer(dst_ids=[dst_id(across), dst_id(far)], dma_engine_mask=out_mask,
                                          remote_sem=s.arrs, srcs=[T.hs[:]], dsts=[T.asc[:], T.osc[:]])],
                       local_sem=s.sent)
    send(partner, T.pc[:].bitcast(u8), T.hc[:].bitcast(u8), s.arrp, rest_mask)
    send(partner, T.ps[:], T.hs[:], s.arrp, rest_mask)
    for k, a, b, bk in halves:
        g.wait_ge(s["arr" + k], n_out)
        send(partner, T.oc[:, a:b].bitcast(u8), T.ac[:, a:b].bitcast(u8), s["onw" + k], chip_mask)
    g.wait_ge(s.sent, 3 * n_out + 2 * n_rest + 2 * n_chip)

    t.wait_ge(s.hqa, 1)
    t.wait_ge(s.hqb, 1)
    t.wait_ge(s.qv, 1)
    t.matmul_mx(bank(0), T.w2c[:], T.w2s[:], T.hc[:], T.hs[:], True, True).then_inc(s.mo, 1)
    t.wait_ge(s.arrp, 2 * n_rest)
    t.matmul_mx(bank(1), T.w2c[:], T.w2s[:], T.pc[:], T.ps[:], True, True).then_inc(s.mp, 1)
    t.wait_ge(s.arra, n_out)
    t.wait_ge(s.arrb, n_out)
    t.wait_ge(s.arrs, 2 * n_out)
    t.matmul_mx(bank(2), T.w2c[:], T.w2s[:], T.ac[:], T.asc[:], True, True).then_inc(s.mc, 1)
    for k, a, b, bk in halves:
        t.wait_ge(s["onw" + k], n_chip)
        t.matmul_mx(bank(3 + bk, HALF), T.w2c[:], T.w2s[:], T.oc[:, a:b], T.osc[:, a:b],
                    True, True).then_inc(s["mf" + k], 1)

    v.wait_ge(s.mo, 1)
    v.tensor_copy(T.yb[:, yblock(core)], bank(0)).then_inc(s.co, 1)
    g.scalar.wait_ge(s.mp, 1)
    g.scalar.activation(T.yb[:, yblock(partner)], bank(1), copy).then_inc(s.cp, 1)
    v.wait_ge(s.mc, 1)
    v.tensor_copy(T.yb[:, yblock(across)], bank(2)).then_inc(s.cc, 1)
    g.scalar.wait_ge(s.mfa, 1)
    g.scalar.activation(T.yb[:, yblock(far, 0, HALF)], bank(3, HALF), copy).then_inc(s.cfa, 1)
    v.wait_ge(s.mfb, 1)
    v.tensor_copy(T.yb[:, yblock(far, HALF, COLS)], bank(7, HALF)).then_inc(s.cfb, 1)

    for sem, cols in ((s.co, yblock(core)), (s.cp, yblock(partner)), (s.cc, yblock(across)),
                      (s.cfa, yblock(far, 0, HALF)), (s.cfb, yblock(far, HALF, COLS))):
        g.sync.wait_ge(sem, 1)
        g.sync.dma_start(T.y[:, cols], T.yb[:, cols]).then_inc(s.st, 16)
    g.sync.wait_ge(s.st, 80)
